import numpy as np
import ml_dtypes


def mxq(x, axis, fmt="e4m3"):
    dtype, down = {"e4m3": (ml_dtypes.float8_e4m3fn, 7), "e5m2": (ml_dtypes.float8_e5m2, 14)}[fmt]
    v = np.moveaxis(np.asarray(x, np.float32).astype(ml_dtypes.bfloat16).astype(np.float64), axis, -1)
    blocks = v.reshape(v.shape[:-1] + (-1, 32))
    amax = np.abs(blocks).max(-1, keepdims=True)
    byte = np.maximum(np.where(amax > 0, np.frexp(amax)[1] - 1 + 127, 0) - down, 1)
    scale = np.exp2(byte - 127.0)
    codes = (blocks / scale).astype(np.float32).astype(dtype).astype(np.float64)
    return np.moveaxis((codes * scale).reshape(v.shape), -1, axis)


WIDE = False


def mx_kscale(k):
    if not WIDE:
        return np.ones(k)
    levels = np.array([10, -10, 5, -5, 0])
    if k % 512:
        return np.exp2(np.random.permutation(np.resize(levels, k // 32))).repeat(32)
    a = np.empty((k // 512, 16))
    for p in range(k // 512):
        a[p, :8] = np.random.permutation(np.resize(levels, 8))
        for g in range(8):
            far = levels[np.abs(levels - a[p, g]) >= 10]
            a[p, g + 8] = far[np.random.randint(len(far))]
    return np.exp2(a.ravel()).repeat(32)


def f64(x):
    return np.asarray(x).astype(np.float64)


def striped(idx):
    return np.tile(idx.reshape(-1, 16).T, (8, 1)).astype(np.uint16)


def unstriped(offs):
    return offs[:16].T.reshape(-1).astype(np.int64)


def relu(v):
    return np.maximum(v, 0.0)


K, T, E, C, H, N = 1536, 1024, 8, 128, 512, 256


def by_expert(wq, xq):
    return np.concatenate([wq[e].T @ xq[:, e * C:(e + 1) * C] for e in range(E)], axis=1)


def setup_inputs():
    n = np.random.standard_normal
    s = mx_kscale(K)[:, None]
    u = mx_kscale(H)
    return {
        "xT": (n((K, T)) * s).astype(np.float32),
        "w1": (n((E, K, H)) / np.sqrt(K) / s[None] * u[None, None, :]).astype(np.float32),
        "w2": (n((E, H, N)) / np.sqrt(H) / u[None, :, None]).astype(np.float32),
        "gate": np.tile(np.random.uniform(0.2, 1.0, E * C), (N, 1)).astype(np.float32),
        "offs": striped(np.random.permutation(T)[:E * C]),
    }


def reference(xT, w1, w2, gate, offs):
    idx = unstriped(offs)
    xq = mxq(f64(xT)[:, idx], 0, "e4m3")
    h = relu(by_expert(mxq(f64(w1), 1, "e4m3"), xq))
    y = by_expert(mxq(f64(w2), 1, "e4m3"), mxq(h, 0, "e4m3"))
    out = np.zeros((N, T))
    out[:, idx] = f64(gate) * y
    return out

@@ -1,0 +1,195 @@
+from contextlib import ExitStack
+
+import concourse.mybir as mybir
+
+K, T, E, C, H, N = 1536, 1024, 8, 128, 512, 256
+FLOPS = 2 * E * C * (K * H + H * N)
+BYTES = 4 * (K * T + E * K * H + E * H * N + E * C + N * T) + 2 * E * C
+
+F32 = mybir.dt.float32
+BF16 = mybir.dt.bfloat16
+U32 = mybir.dt.uint32
+U16 = mybir.dt.uint16
+U8 = mybir.dt.uint8
+FP8X4 = mybir.dt.float8_e4m3fn_x4
+MULT = mybir.AluOpType.mult
+RELU = mybir.ActivationFunctionType.Relu
+
+P = 128
+PASSES = K // 512
+HALF = 512
+
+
+def tile_routed_moe_kernel(tc, xT, w1, w2, gate, offs, out):
+    nc = tc.nc
+    with ExitStack() as ctx:
+        keep = ctx.enter_context(tc.tile_pool(name="keep", bufs=1))
+        rawp = ctx.enter_context(tc.tile_pool(name="rawp", bufs=11))
+        raw2p = ctx.enter_context(tc.tile_pool(name="raw2p", bufs=3))
+        grp = ctx.enter_context(tc.tile_pool(name="grp", bufs=6))
+        w1p = ctx.enter_context(tc.tile_pool(name="w1p", bufs=9))
+        w2p = ctx.enter_context(tc.tile_pool(name="w2p", bufs=3))
+        hp = ctx.enter_context(tc.tile_pool(name="hp", bufs=3))
+        psum = ctx.enter_context(tc.psum_pool(name="psum", bufs=3))
+
+        offs_t = keep.tile([P, E * C // 16], U16, name="offs_t")
+        nc.sync.dma_start(offs_t[:], offs)
+        gate_t = keep.tile([P, E * C], F32, name="gate_t")
+        window = [keep.tile([P, T], F32, name=f"window{b}") for b in range(2)]
+        x_codes = [keep.tile([P, T], U32, name=f"x_codes{g}", align_bytes=64) for g in range(PASSES)]
+        x_scales = keep.tile([P, T], U8, name="x_scales", align_bytes=64)
+        nc.gpsimd.memset(x_scales[:], 0)
+        slot_codes = [[keep.tile([P, HALF], U32, name=f"slot_codes{g}_{s}", align_bytes=64) for s in range(2)] for g in range(PASSES)]
+        slot_scales = [keep.tile([P, HALF], U8, name=f"slot_scales{s}", align_bytes=64) for s in range(2)]
+
+        w1_codes, w1_scales, w2_codes, w2_scales = {}, {}, {}, {}
+        h_psum, y_sb, hb, hc, hs = {}, {}, {}, {}, {}
+
+        def load_and_group(job, share):
+            kind, a, b = job
+            if kind == "x":
+                raw = rawp.tile([P, 4, 512], F32, name="raw", tag="raw")
+                nc.sync.dma_start(raw[:], xT[512 * a : 512 * (a + 1), HALF * b : HALF * (b + 1)].rearrange("(p j) n -> p j n", j=4))
+                width = 512
+            elif kind == "w1":
+                raw = rawp.tile([P, 4, 512], F32, name="raw", tag="raw")
+                nc.sync.dma_start(raw[:], w1[a, 512 * b : 512 * (b + 1), :].rearrange("(p j) n -> p j n", j=4))
+                width = 512
+            else:
+                raw = raw2p.tile([P, 4, 256], F32, name="raw2", tag="raw2")
+                nc.sync.dma_start(raw[:], w2[a].rearrange("(p j) n -> p j n", j=4))
+                width = 256
+            grouped = grp.tile([P, 4 * width], BF16, name="grouped", tag="grouped", align_bytes=64)
+            if kind == "w1":
+                dst = grouped[:].rearrange("p (t m j) -> p m j t", t=4, j=4)
+                src = raw[:].rearrange("p j (m t) -> p m j t", t=4)
+            else:
+                dst = grouped[:].rearrange("p (c i j) -> p c j i", i=4, j=4)
+                src = raw[:].rearrange("p j (c i) -> p c j i", i=4)
+            cut = int(width // 4 * share) // 4 * 4
+            if cut > 0:
+                nc.scalar.copy(dst[:, :cut], src[:, :cut])
+            if cut < width // 4:
+                nc.vector.tensor_copy(dst[:, cut:], src[:, cut:])
+            return grouped
+
+        def quantise(job, grouped):
+            kind, a, b = job
+            if kind == "x":
+                cols = slice(HALF * b, HALF * (b + 1))
+                codes, scales = x_codes[a][:, cols], x_scales[4 * a : P, cols]
+            elif kind == "w1":
+                w1_codes[a, b] = w1p.tile([P, 512], U32, name="w1_codes", tag="w1_codes", align_bytes=64)
+                w1_scales[a, b] = w1p.tile([P, 512], U8, name="w1_scales", tag="w1_scales", align_bytes=64)
+                codes, scales = w1_codes[a, b][:], w1_scales[a, b][:]
+            else:
+                w2_codes[a] = w2p.tile([P, 256], U32, name="w2_codes", tag="w2_codes", align_bytes=64)
+                w2_scales[a] = w2p.tile([P, 256], U8, name="w2_scales", tag="w2_scales", align_bytes=64)
+                codes, scales = w2_codes[a][:], w2_scales[a][:]
+            nc.vector.quantize_mx(out=codes.bitcast(FP8X4), scales=scales, in_=grouped[:])
+
+        def gather_codes(g, s):
+            cols = slice(HALF // 16 * s, HALF // 16 * (s + 1))
+            nc.vector.tensor_copy(slot_codes[g][s][:], x_codes[g][:].indirect(offs_t[:, cols]))
+
+        def gather_scales(s):
+            cols = slice(HALF // 16 * s, HALF // 16 * (s + 1))
+            nc.vector.tensor_copy(slot_scales[s][:], x_scales[:].indirect(offs_t[:, cols]))
+
+        def layer1(e):
+            h_psum[e] = psum.tile([P, 4, C], F32, name="h_psum", tag="h_psum")
+            cols = slice(C * (e % 4), C * (e % 4 + 1))
+            for t in range(4):
+                for g in range(PASSES):
+                    nc.tensor.matmul_mx(
+                        out=h_psum[e][:, t, :],
+                        lhsT=w1_codes[e, g][:, 128 * t : 128 * (t + 1)].bitcast(FP8X4),
+                        lhsT_scale=w1_scales[e, g][:, 128 * t : 128 * (t + 1)],
+                        rhs=slot_codes[g][e // 4][:, cols].bitcast(FP8X4),
+                        rhs_scale=slot_scales[e // 4][4 * g : P, cols],
+                        start=(g == 0),
+                        stop=(g == PASSES - 1),
+                    )
+
+        def hidden(e):
+            hb[e] = hp.tile([P, C, 4], BF16, name="hb", tag="hb", align_bytes=64)
+            nc.scalar.activation(hb[e][:], h_psum[e][:].rearrange("p t n -> p n t"), RELU)
+
+        def quantise_hidden(e):
+            hc[e] = hp.tile([P, C], U32, name="hc", tag="hc", align_bytes=64)
+            hs[e] = hp.tile([P, C], U8, name="hs", tag="hs", align_bytes=64)
+            nc.vector.quantize_mx(out=hc[e][:].bitcast(FP8X4), scales=hs[e][:], in_=hb[e][:].rearrange("p n t -> p (n t)"))
+
+        def layer2(e):
+            y_psum = psum.tile([P, 2, C], F32, name="y_psum", tag="y_psum")
+            for b in range(2):
+                nc.tensor.matmul_mx(
+                    out=y_psum[:, b, :],
+                    lhsT=w2_codes[e][:, 128 * b : 128 * (b + 1)].bitcast(FP8X4),
+                    lhsT_scale=w2_scales[e][:, 128 * b : 128 * (b + 1)],
+                    rhs=hc[e][:].bitcast(FP8X4),
+                    rhs_scale=hs[e][:],
+                    start=True,
+                    stop=True,
+                )
+            y_sb[e] = hp.tile([P, 2, C], F32, name="y_sb", tag="y_sb")
+            nc.scalar.copy(y_sb[e][:], y_psum[:])
+
+        def scatter(e, b):
+            nc.vector.tensor_tensor(
+                window[b][:].indirect(offs_t[:, C // 16 * e : C // 16 * (e + 1)]),
+                y_sb[e][:, b, :],
+                gate_t[:, C * e : C * (e + 1)],
+                MULT,
+            )
+
+        jobs = [(("x", g, s), 0.0 if (g, s) == (1, 0) else 1.0) for g in range(PASSES) for s in range(2)]
+        w1_share = [1.0, 0.0, 1.0]
+        for e in range(E - 2):
+            jobs += [(("w1", e, g), w1_share[g]) for g in range(PASSES)] + [(("w2", e, 0), 0.0)]
+        jobs += [(("w1", e, g), w1_share[g]) for e in (E - 2, E - 1) for g in range(PASSES)]
+        jobs[-1] = (jobs[-1][0], 0.375)
+        jobs += [(("w2", E - 2, 0), 0.0), (("w2", E - 1, 0), 0.375)]
+
+        waiting = []
+
+        def quantise_and_follow(job, grouped):
+            kind, a, b = job
+            quantise(job, grouped)
+            if waiting:
+                step = waiting.pop(0)
+                step[0](*step[1:])
+            if kind == "x" and b == 1:
+                gather_codes(a, 0)
+                if a == PASSES - 1:
+                    gather_scales(0)
+            if kind == "w1" and b == PASSES - 1:
+                layer1(a)
+                waiting.append((hidden, a))
+                waiting.append((quantise_hidden, a))
+                if a in (1, 2):
+                    gather_codes(a - 1, 1)
+                if a == 3:
+                    gather_codes(2, 1)
+                    gather_scales(1)
+            if kind == "w2":
+                waiting.append((finish, a))
+
+        def finish(e):
+            layer2(e)
+            scatter(e, 0)
+            scatter(e, 1)
+
+        pending = None
+        for job, share in jobs:
+            grouped = load_and_group(job, share)
+            if pending:
+                quantise_and_follow(*pending)
+            pending = (job, grouped)
+            if job == ("w2", 0, 0):
+                nc.sync.dma_start(gate_t[:], gate[0:P, :])
+        quantise_and_follow(*pending)
+        for step in waiting:
+            step[0](*step[1:])
+        for b in range(2):
+            nc.sync.dma_start(out[P * b : P * (b + 1), :], window[b][:])

@@ -15,6 +15,7 @@ FP8X4 = mybir.dt.float8_e4m3fn_x4
 MULT = mybir.AluOpType.mult
 RELU = mybir.ActivationFunctionType.Relu
 
+CFG = {"x": [0.75,0,0.75,0.5,0.375,0.75],"w1": [1,1,0.625,0.5,0.375,0],"w1_tail": [1,1,0.625,0.625,0,1],"w2": 1,"w2_tail": [0.375,0.5],"relu": 0,"qh": 0,"l2": 1,"yc": 1,"sc": 5,"trelu": 0,"tqh": 1,"tl2": 1,"tyc": 1,"tsc": 4,"g1": [9,3,9,0],"w2pos": [2,0],"first": 0,"qd": 0,"xwhole": 1,"rawb": 8,"gpos": [9,13,26,32],"w2d": 0,"yV": 1,"tyV": 0,"rV": [0,1],"trV": [0,0]}
 P = 128
 PASSES = K // 512
 HALF = 512
@@ -24,13 +25,13 @@ def tile_routed_moe_kernel(tc, xT, w1, w2, gate, offs, out):
     nc = tc.nc
     with ExitStack() as ctx:
         keep = ctx.enter_context(tc.tile_pool(name="keep", bufs=1))
-        rawp = ctx.enter_context(tc.tile_pool(name="rawp", bufs=11))
-        raw2p = ctx.enter_context(tc.tile_pool(name="raw2p", bufs=3))
-        grp = ctx.enter_context(tc.tile_pool(name="grp", bufs=6))
-        w1p = ctx.enter_context(tc.tile_pool(name="w1p", bufs=9))
-        w2p = ctx.enter_context(tc.tile_pool(name="w2p", bufs=3))
-        hp = ctx.enter_context(tc.tile_pool(name="hp", bufs=3))
-        psum = ctx.enter_context(tc.psum_pool(name="psum", bufs=3))
+        rawp = ctx.enter_context(tc.tile_pool(name="rawp", bufs=CFG["rawb"]))
+        rawxp = ctx.enter_context(tc.tile_pool(name="rawxp", bufs=2))
+        grp = ctx.enter_context(tc.tile_pool(name="grp", bufs=4))
+        w1p = ctx.enter_context(tc.tile_pool(name="w1p", bufs=5))
+        w2p = ctx.enter_context(tc.tile_pool(name="w2p", bufs=2))
+        hp = ctx.enter_context(tc.tile_pool(name="hp", bufs=2))
+        psum = ctx.enter_context(tc.psum_pool(name="psum", bufs=4))
 
         offs_t = keep.tile([P, E * C // 16], U16, name="offs_t")
         nc.sync.dma_start(offs_t[:], offs)
@@ -42,51 +43,72 @@ def tile_routed_moe_kernel(tc, xT, w1, w2, gate, offs, out):
         slot_codes = [[keep.tile([P, HALF], U32, name=f"slot_codes{g}_{s}", align_bytes=64) for s in range(2)] for g in range(PASSES)]
         slot_scales = [keep.tile([P, HALF], U8, name=f"slot_scales{s}", align_bytes=64) for s in range(2)]
 
-        w1_codes, w1_scales, w2_codes, w2_scales = {}, {}, {}, {}
-        h_psum, y_sb, hb, hc, hs = {}, {}, {}, {}, {}
+        x_raw, w1_ops, w2_ops = {}, {}, {}
+        h_psum, y_psum, y_sb, hb, hc, hs = {}, {}, {}, {}, {}, {}
 
-        def load_and_group(job, share):
+        def load_and_group(job, share, grouped, at, width):
             kind, a, b = job
             if kind == "x":
-                raw = rawp.tile([P, 4, 512], F32, name="raw", tag="raw")
-                nc.sync.dma_start(raw[:], xT[512 * a : 512 * (a + 1), HALF * b : HALF * (b + 1)].rearrange("(p j) n -> p j n", j=4))
-                width = 512
+                if CFG["xwhole"]:
+                    if b == 0:
+                        x_raw[a] = rawxp.tile([P, 4, T], F32, name="x_raw", tag="x_raw")
+                        nc.sync.dma_start(x_raw[a][:], xT[512 * a : 512 * (a + 1), :].rearrange("(p j) n -> p j n", j=4))
+                    raw = x_raw[a][:, :, HALF * b : HALF * (b + 1)]
+                else:
+                    raw = rawp.tile([P, 4, 512], F32, name="raw", tag="raw")
+                    nc.sync.dma_start(raw[:], xT[512 * a : 512 * (a + 1), HALF * b : HALF * (b + 1)].rearrange("(p j) n -> p j n", j=4))
             elif kind == "w1":
                 raw = rawp.tile([P, 4, 512], F32, name="raw", tag="raw")
                 nc.sync.dma_start(raw[:], w1[a, 512 * b : 512 * (b + 1), :].rearrange("(p j) n -> p j n", j=4))
-                width = 512
             else:
-                raw = raw2p.tile([P, 4, 256], F32, name="raw2", tag="raw2")
-                nc.sync.dma_start(raw[:], w2[a].rearrange("(p j) n -> p j n", j=4))
-                width = 256
-            grouped = grp.tile([P, 4 * width], BF16, name="grouped", tag="grouped", align_bytes=64)
+                raw = rawp.tile([P, 4 * width], F32, name="raw", tag="raw")
+                for k in range(b):
+                    nc.sync.dma_start(raw[:, 1024 * k : 1024 * (k + 1)], w2[a + k].rearrange("(p j) n -> p (j n)", j=4))
+            whole = grouped[:, at : at + 4 * width]
             if kind == "w1":
-                dst = grouped[:].rearrange("p (t m j) -> p m j t", t=4, j=4)
-                src = raw[:].rearrange("p j (m t) -> p m j t", t=4)
+                dst = whole.rearrange("p (t m j) -> p m j t", t=4, j=4)
+                src = raw[:, :, :].rearrange("p j (m t) -> p m j t", t=4)
+            elif kind == "x":
+                dst = whole.rearrange("p (c i j) -> p c j i", i=4, j=4)
+                src = raw[:, :, :].rearrange("p j (c i) -> p c j i", i=4)
             else:
-                dst = grouped[:].rearrange("p (c i j) -> p c j i", i=4, j=4)
-                src = raw[:].rearrange("p j (c i) -> p c j i", i=4)
+                dst = whole.rearrange("p (e c i j) -> p e c j i", e=b, i=4, j=4)
+                src = raw[:].rearrange("p (e j c i) -> p e c j i", e=b, i=4, j=4)
+                if share == 0.5 and b == 2:
+                    nc.scalar.copy(dst[:, 0], src[:, 0])
+                    nc.vector.tensor_copy(dst[:, 1], src[:, 1])
+                    return
+                for k in range(b):
+                    cut = int(64 * share) // 4 * 4
+                    if cut > 0:
+                        nc.scalar.copy(dst[:, k, :cut], src[:, k, :cut])
+                    if cut < 64:
+                        nc.vector.tensor_copy(dst[:, k, cut:], src[:, k, cut:])
+                return
             cut = int(width // 4 * share) // 4 * 4
             if cut > 0:
                 nc.scalar.copy(dst[:, :cut], src[:, :cut])
             if cut < width // 4:
                 nc.vector.tensor_copy(dst[:, cut:], src[:, cut:])
-            return grouped
 
-        def quantise(job, grouped):
-            kind, a, b = job
+        def quantise(group, grouped, width):
+            kind, a, b = group[0][0]
             if kind == "x":
-                cols = slice(HALF * b, HALF * (b + 1))
+                cols = slice(HALF * b, HALF * b + width)
                 codes, scales = x_codes[a][:, cols], x_scales[4 * a : P, cols]
             elif kind == "w1":
-                w1_codes[a, b] = w1p.tile([P, 512], U32, name="w1_codes", tag="w1_codes", align_bytes=64)
-                w1_scales[a, b] = w1p.tile([P, 512], U8, name="w1_scales", tag="w1_scales", align_bytes=64)
-                codes, scales = w1_codes[a, b][:], w1_scales[a, b][:]
+                codes = w1p.tile([P, width], U32, name="w1_codes", tag="w1_codes", align_bytes=64)
+                scales = w1p.tile([P, width], U8, name="w1_scales", tag="w1_scales", align_bytes=64)
+                for k, (job, share) in enumerate(group):
+                    w1_ops[job[1], job[2]] = (codes, scales, 512 * k)
+                codes, scales = codes[:], scales[:]
             else:
-                w2_codes[a] = w2p.tile([P, 256], U32, name="w2_codes", tag="w2_codes", align_bytes=64)
-                w2_scales[a] = w2p.tile([P, 256], U8, name="w2_scales", tag="w2_scales", align_bytes=64)
-                codes, scales = w2_codes[a][:], w2_scales[a][:]
-            nc.vector.quantize_mx(out=codes.bitcast(FP8X4), scales=scales, in_=grouped[:])
+                codes = w2p.tile([P, width], U32, name="w2_codes", tag="w2_codes", align_bytes=64)
+                scales = w2p.tile([P, width], U8, name="w2_scales", tag="w2_scales", align_bytes=64)
+                for k in range(b):
+                    w2_ops[a + k] = (codes, scales, 256 * k)
+                codes, scales = codes[:], scales[:]
+            nc.vector.quantize_mx(out=codes.bitcast(FP8X4), scales=scales, in_=grouped[:, : 4 * width])
 
         def gather_codes(g, s):
             cols = slice(HALF // 16 * s, HALF // 16 * (s + 1))
@@ -101,95 +123,156 @@ def tile_routed_moe_kernel(tc, xT, w1, w2, gate, offs, out):
             cols = slice(C * (e % 4), C * (e % 4 + 1))
             for t in range(4):
                 for g in range(PASSES):
+                    codes, scales, at = w1_ops[e, g]
                     nc.tensor.matmul_mx(
                         out=h_psum[e][:, t, :],
-                        lhsT=w1_codes[e, g][:, 128 * t : 128 * (t + 1)].bitcast(FP8X4),
-                        lhsT_scale=w1_scales[e, g][:, 128 * t : 128 * (t + 1)],
+                        lhsT=codes[:, at + 128 * t : at + 128 * (t + 1)].bitcast(FP8X4),
+                        lhsT_scale=scales[:, at + 128 * t : at + 128 * (t + 1)],
                         rhs=slot_codes[g][e // 4][:, cols].bitcast(FP8X4),
                         rhs_scale=slot_scales[e // 4][4 * g : P, cols],
                         start=(g == 0),
                         stop=(g == PASSES - 1),
                     )
 
-        def hidden(e):
-            hb[e] = hp.tile([P, C, 4], BF16, name="hb", tag="hb", align_bytes=64)
-            nc.scalar.activation(hb[e][:], h_psum[e][:].rearrange("p t n -> p n t"), RELU)
+        def hidden(e, n):
+            if e % n == 0:
+                hb[e] = hp.tile([P, C * n, 4], BF16, name="hb", tag="hb", align_bytes=64)
+            k = e % n
+            dst = hb[e - k][:, C * k : C * (k + 1), :]
+            src = h_psum[e][:].rearrange("p t n -> p n t")
+            if CFG["trV" if e >= E - 2 else "rV"][e % 2]:
+                nc.vector.tensor_scalar_max(dst, src, 0.0)
+            else:
+                nc.scalar.activation(dst, src, RELU)
 
-        def quantise_hidden(e):
-            hc[e] = hp.tile([P, C], U32, name="hc", tag="hc", align_bytes=64)
-            hs[e] = hp.tile([P, C], U8, name="hs", tag="hs", align_bytes=64)
+        def quantise_hidden(e, n):
+            hc[e] = hp.tile([P, C * n], U32, name="hc", tag="hc", align_bytes=64)
+            hs[e] = hp.tile([P, C * n], U8, name="hs", tag="hs", align_bytes=64)
             nc.vector.quantize_mx(out=hc[e][:].bitcast(FP8X4), scales=hs[e][:], in_=hb[e][:].rearrange("p n t -> p (n t)"))
 
-        def layer2(e):
-            y_psum = psum.tile([P, 2, C], F32, name="y_psum", tag="y_psum")
+        def layer2(e, n):
+            y_psum[e] = psum.tile([P, 2, C * n], F32, name="y_psum", tag="y_psum")
             for b in range(2):
-                nc.tensor.matmul_mx(
-                    out=y_psum[:, b, :],
-                    lhsT=w2_codes[e][:, 128 * b : 128 * (b + 1)].bitcast(FP8X4),
-                    lhsT_scale=w2_scales[e][:, 128 * b : 128 * (b + 1)],
-                    rhs=hc[e][:].bitcast(FP8X4),
-                    rhs_scale=hs[e][:],
-                    start=True,
-                    stop=True,
-                )
-            y_sb[e] = hp.tile([P, 2, C], F32, name="y_sb", tag="y_sb")
-            nc.scalar.copy(y_sb[e][:], y_psum[:])
+                for k in range(n):
+                    codes, scales, at = w2_ops[e + k]
+                    nc.tensor.matmul_mx(
+                        out=y_psum[e][:, b, C * k : C * (k + 1)],
+                        lhsT=codes[:, at + 128 * b : at + 128 * (b + 1)].bitcast(FP8X4),
+                        lhsT_scale=scales[:, at + 128 * b : at + 128 * (b + 1)],
+                        rhs=hc[e][:, C * k : C * (k + 1)].bitcast(FP8X4),
+                        rhs_scale=hs[e][:, C * k : C * (k + 1)],
+                        start=True,
+                        stop=True,
+                    )
 
-        def scatter(e, b):
+        def y_out(e, n):
+            y_sb[e] = hp.tile([P, 2, C * n], F32, name="y_sb", tag="y_sb")
+            if CFG["tyV" if e >= E - 2 else "yV"]:
+                nc.vector.tensor_copy(y_sb[e][:], y_psum[e][:])
+            else:
+                nc.scalar.copy(y_sb[e][:], y_psum[e][:])
+
+        def scatter(e, n, b):
             nc.vector.tensor_tensor(
-                window[b][:].indirect(offs_t[:, C // 16 * e : C // 16 * (e + 1)]),
+                window[b][:].indirect(offs_t[:, C // 16 * e : C // 16 * (e + n)]),
                 y_sb[e][:, b, :],
-                gate_t[:, C * e : C * (e + 1)],
+                gate_t[:, C * e : C * (e + n)],
                 MULT,
             )
 
-        jobs = [(("x", g, s), 0.0 if (g, s) == (1, 0) else 1.0) for g in range(PASSES) for s in range(2)]
-        w1_share = [1.0, 0.0, 1.0]
-        for e in range(E - 2):
-            jobs += [(("w1", e, g), w1_share[g]) for g in range(PASSES)] + [(("w2", e, 0), 0.0)]
-        jobs += [(("w1", e, g), w1_share[g]) for e in (E - 2, E - 1) for g in range(PASSES)]
-        jobs[-1] = (jobs[-1][0], 0.375)
-        jobs += [(("w2", E - 2, 0), 0.0), (("w2", E - 1, 0), 0.375)]
+        xs = [[(("x", g, s), CFG["x"][2 * g + s])] for g in range(PASSES) for s in range(2)]
+        weights = []
+        for pair in range(E // 2):
+            last = pair == E // 2 - 1
+            share = CFG["w1_tail"] if last else CFG["w1"]
+            tiles = [(("w1", 2 * pair + q // 3, q % 3), share[q]) for q in range(6)]
+            weights += [tiles[0:2], tiles[2:4]] + ([tiles[4:5], tiles[5:6]] if last else [tiles[4:6]])
+        for pair in reversed(range(E // 2 - 1)):
+            weights.insert(min(3 * (pair + 1) + CFG["w2d"], len(weights)), [(("w2", 2 * pair, 2), CFG["w2"])])
+        n = len(weights)
+        if CFG["w2pos"][0] == CFG["w2pos"][1]:
+            weights.insert(n - CFG["w2pos"][0], [(("w2", E - 2, 2), CFG["w2_tail"][1])])
+        else:
+            weights.insert(n - CFG["w2pos"][0], [(("w2", E - 2, 1), CFG["w2_tail"][0])])
+            weights.insert(n + 1 - CFG["w2pos"][1], [(("w2", E - 1, 1), CFG["w2_tail"][1])])
+        first = CFG["first"]
+        groups = weights[:first] + xs + weights[first:]
 
-        waiting = []
+        due = []
+        count = [0]
+        done = {}
 
-        def quantise_and_follow(job, grouped):
-            kind, a, b = job
-            quantise(job, grouped)
-            if waiting:
-                step = waiting.pop(0)
-                step[0](*step[1:])
+        def at(i, f, *args):
+            count[0] += 1
+            due.append((i, count[0], f, args))
+
+        def run_due(i):
+            while True:
+                ready = sorted(d for d in due if d[0] <= i)
+                if not ready:
+                    return
+                d = ready[0]
+                due.remove(d)
+                d[2](*d[3])
+
+        def follow(i, group):
+            kind, a, b = group[-1][0]
             if kind == "x" and b == 1:
                 gather_codes(a, 0)
                 if a == PASSES - 1:
                     gather_scales(0)
-            if kind == "w1" and b == PASSES - 1:
-                layer1(a)
-                waiting.append((hidden, a))
-                waiting.append((quantise_hidden, a))
-                if a in (1, 2):
-                    gather_codes(a - 1, 1)
-                if a == 3:
-                    gather_codes(2, 1)
-                    gather_scales(1)
-            if kind == "w2":
-                waiting.append((finish, a))
+                    for k in range(3):
+                        at(i + CFG["g1"][k], gather_codes, k, 1)
+                    at(i + CFG["g1"][3], gather_scales, 1)
+            for e in range(E):
+                tail = e >= E - 2
+                t = "t" if tail else ""
+                width = 1 if tail else 2
+                lead = e if tail else e // 2 * 2
+                if all((e, g) in w1_ops for g in range(PASSES)) and ("l1", e) not in done and x_ready[0]:
+                    done["l1", e] = i + CFG[t + "relu"]
+                    layer1(e)
+                    at(done["l1", e], hidden, e, width)
+                    if e == lead + width - 1:
+                        done["q", lead] = i + CFG[t + "qh"]
+                        at(i + CFG[t + "qh"], quantise_hidden, lead, width)
+                if ("q", lead) in done and all(lead + k in w2_ops for k in range(width)) and ("l2", lead) not in done:
+                    base = max(i, done["q", lead])
+                    done["l2", lead] = base
+                    at(base + CFG[t + "l2"] - CFG[t + "qh"], layer2, lead, width)
+                    at(base + CFG[t + "yc"] - CFG[t + "qh"], y_out, lead, width)
+                    at(base + CFG[t + "sc"] - CFG[t + "qh"], scatter, lead, width, 0)
+                    at(base + CFG[t + "sc"] - CFG[t + "qh"], scatter, lead, width, 1)
 
-        def finish(e):
-            layer2(e)
-            scatter(e, 0)
-            scatter(e, 1)
-
-        pending = None
-        for job, share in jobs:
-            grouped = load_and_group(job, share)
-            if pending:
-                quantise_and_follow(*pending)
-            pending = (job, grouped)
-            if job == ("w2", 0, 0):
-                nc.sync.dma_start(gate_t[:], gate[0:P, :])
-        quantise_and_follow(*pending)
-        for step in waiting:
-            step[0](*step[1:])
+        x_ready = [0]
+        i = 0
+        queue = []
+        for group in groups:
+            kind = group[0][0][0]
+            width = 512 if kind != "w2" else 256 * group[0][0][2]
+            grouped = grp.tile([P, 4096], BF16, name="grouped", tag="grouped", align_bytes=64)
+            for k, (job, share) in enumerate(group):
+                load_and_group(job, share, grouped, 2048 * k, width)
+                for pair in range(E // 2):
+                    if i == CFG["gpos"][pair]:
+                        cols = slice(2 * C * pair, 2 * C * (pair + 1))
+                        nc.sync.dma_start(gate_t[:, cols], gate[0:P, cols])
+                if len(queue) > CFG["qd"]:
+                    g = queue.pop(0)
+                    quantise(*g)
+                    if g[0][0][0] == ("x", PASSES - 1, 1):
+                        x_ready[0] = 1
+                    run_due(i)
+                    follow(i, g[0])
+                else:
+                    run_due(i)
+                i += 1
+            queue.append((group, grouped, width * len(group)))
+        for g in queue:
+            quantise(*g)
+            run_due(i)
+            follow(i, g[0])
+            i += 1
+        run_due(1000)
         for b in range(2):
             nc.sync.dma_start(out[P * b : P * (b + 1), :], window[b][:])

@@ -15,7 +15,7 @@ FP8X4 = mybir.dt.float8_e4m3fn_x4
 MULT = mybir.AluOpType.mult
 RELU = mybir.ActivationFunctionType.Relu
 
-CFG = {"x": [0.75,0,0.75,0.5,0.375,0.75],"w1": [1,1,0.625,0.5,0.375,0],"w1_tail": [1,1,0.625,0.625,0,1],"w2": 1,"w2_tail": [0.375,0.5],"relu": 0,"qh": 0,"l2": 1,"yc": 1,"sc": 5,"trelu": 0,"tqh": 1,"tl2": 1,"tyc": 1,"tsc": 4,"g1": [9,3,9,0],"w2pos": [2,0],"first": 0,"qd": 0,"xwhole": 1,"rawb": 8,"gpos": [9,13,26,32],"w2d": 0,"yV": 1,"tyV": 0,"rV": [0,1],"trV": [0,0]}
+CFG = {"x": [0.5,0.375,0.625,0.375,0.125,0.375],"w1": [1,1,0.6875,1,0.3125,0],"w1_tail": [0.625,1,1,1,0.4375,1],"w2": 1,"w2_tail": [1,1],"relu": 0,"qh": 2,"l2": 4,"yc": 4,"sc": 8,"trelu": 1,"tqh": 1,"tl2": 2,"tyc": 3,"tsc": 5,"g1": [5,6,8,8],"first": 0,"qd": 0,"rawb": 10,"gpos": [15,24,28,21],"w2d": 0,"yV": 1,"tyV": 0,"rV": [0,1],"trV": [0,0],"hb": 4,"gpe": 1,"split": 0,"order": [0,1,4,2,3,5],"lw": 1,"x0": [256,256,512],"xw": 1024,"w2one": 1}
 P = 128
 PASSES = K // 512
 HALF = 512
@@ -31,10 +31,18 @@ def tile_routed_moe_kernel(tc, xT, w1, w2, gate, offs, out):
         w1p = ctx.enter_context(tc.tile_pool(name="w1p", bufs=5))
         w2p = ctx.enter_context(tc.tile_pool(name="w2p", bufs=2))
         hp = ctx.enter_context(tc.tile_pool(name="hp", bufs=2))
-        psum = ctx.enter_context(tc.psum_pool(name="psum", bufs=4))
+        psum_h = ctx.enter_context(tc.psum_pool(name="psum_h", bufs=CFG["hb"]))
+        psum_y = ctx.enter_context(tc.psum_pool(name="psum_y", bufs=3))
 
         offs_t = keep.tile([P, E * C // 16], U16, name="offs_t")
         nc.sync.dma_start(offs_t[:], offs)
+        if CFG["gpe"]:
+            gate_row = keep.tile([P, E * C], F32, name="gate_row")
+            nc.gpsimd.memset(gate_row[:], 0.0)
+            nc.sync.dma_start(gate_row[0:1, :], gate[0:1, :])
+            pick = keep.tile([P, P], F32, name="pick")
+            nc.gpsimd.memset(pick[:], 0.0)
+            nc.gpsimd.memset(pick[0:1, :], 1.0)
         gate_t = keep.tile([P, E * C], F32, name="gate_t")
         window = [keep.tile([P, T], F32, name=f"window{b}") for b in range(2)]
         x_codes = [keep.tile([P, T], U32, name=f"x_codes{g}", align_bytes=64) for g in range(PASSES)]
@@ -46,24 +54,41 @@ def tile_routed_moe_kernel(tc, xT, w1, w2, gate, offs, out):
         x_raw, w1_ops, w2_ops = {}, {}, {}
         h_psum, y_psum, y_sb, hb, hc, hs = {}, {}, {}, {}, {}, {}
 
-        def load_and_group(job, share, grouped, at, width):
-            kind, a, b = job
+        def load(group):
+            kind, a, b = group[0][0][:3]
             if kind == "x":
-                if CFG["xwhole"]:
-                    if b == 0:
-                        x_raw[a] = rawxp.tile([P, 4, T], F32, name="x_raw", tag="x_raw")
-                        nc.sync.dma_start(x_raw[a][:], xT[512 * a : 512 * (a + 1), :].rearrange("(p j) n -> p j n", j=4))
-                    raw = x_raw[a][:, :, HALF * b : HALF * (b + 1)]
-                else:
-                    raw = rawp.tile([P, 4, 512], F32, name="raw", tag="raw")
-                    nc.sync.dma_start(raw[:], xT[512 * a : 512 * (a + 1), HALF * b : HALF * (b + 1)].rearrange("(p j) n -> p j n", j=4))
+                if b not in x_load[a]:
+                    return x_raw[a, b][0][:, :, x_raw[a, b][1] : x_raw[a, b][1] + group[0][0][3]]
+                n = x_load[a][b]
+                pool = rawp if n <= 512 or CFG["lw"] == 2 else rawxp
+                raw = pool.tile([P, 4, n], F32, name="raw", tag="raw")
+                nc.sync.dma_start(raw[:], xT[512 * a : 512 * (a + 1), b : b + n].rearrange("(p j) n -> p j n", j=4))
+                for c in range(b, b + n, 256):
+                    x_raw[a, c] = (raw, c - b)
+                return raw[:, :, 0 : group[0][0][3]]
+            if kind == "w1":
+                raws = []
+                step = CFG["lw"] if len(group) == 2 else 1
+                for k in range(0, len(group), step):
+                    raw = rawp.tile([P, step, 4, 512], F32, name="raw", tag="raw")
+                    row = 512 * (PASSES * a + b + k)
+                    nc.sync.dma_start(raw[:], w1.rearrange("e k n -> (e k) n")[row : row + 512 * step, :].rearrange("(u p j) n -> p u j n", u=step, j=4))
+                    raws += [raw[:, u] for u in range(step)]
+                return raws
+            if kind == "w2":
+                raw = rawp.tile([P, b * 1024], F32, name="raw", tag="raw")
+                nc.sync.dma_start(raw[:].rearrange("p (e m) -> p e m", e=b), w2[a : a + b].rearrange("e (p j) n -> p e (j n)", j=4))
+                return raw
+            return None
+
+        def load_and_group(job, share, grouped, at, width, group_raw):
+            kind, a, b = job[:3]
+            if kind == "x":
+                raw = group_raw
             elif kind == "w1":
-                raw = rawp.tile([P, 4, 512], F32, name="raw", tag="raw")
-                nc.sync.dma_start(raw[:], w1[a, 512 * b : 512 * (b + 1), :].rearrange("(p j) n -> p j n", j=4))
+                raw = group_raw[at // 2048]
             else:
-                raw = rawp.tile([P, 4 * width], F32, name="raw", tag="raw")
-                for k in range(b):
-                    nc.sync.dma_start(raw[:, 1024 * k : 1024 * (k + 1)], w2[a + k].rearrange("(p j) n -> p (j n)", j=4))
+                raw = group_raw[:, :]
             whole = grouped[:, at : at + 4 * width]
             if kind == "w1":
                 dst = whole.rearrange("p (t m j) -> p m j t", t=4, j=4)
@@ -77,6 +102,10 @@ def tile_routed_moe_kernel(tc, xT, w1, w2, gate, offs, out):
                 if share == 0.5 and b == 2:
                     nc.scalar.copy(dst[:, 0], src[:, 0])
                     nc.vector.tensor_copy(dst[:, 1], src[:, 1])
+                    return
+                if share in (0.0, 1.0) and CFG["w2one"]:
+                    copy = nc.scalar.copy if share else nc.vector.tensor_copy
+                    copy(dst, src)
                     return
                 for k in range(b):
                     cut = int(64 * share) // 4 * 4
@@ -92,9 +121,9 @@ def tile_routed_moe_kernel(tc, xT, w1, w2, gate, offs, out):
                 nc.vector.tensor_copy(dst[:, cut:], src[:, cut:])
 
         def quantise(group, grouped, width):
-            kind, a, b = group[0][0]
+            kind, a, b = group[0][0][:3]
             if kind == "x":
-                cols = slice(HALF * b, HALF * b + width)
+                cols = slice(b, b + width)
                 codes, scales = x_codes[a][:, cols], x_scales[4 * a : P, cols]
             elif kind == "w1":
                 codes = w1p.tile([P, width], U32, name="w1_codes", tag="w1_codes", align_bytes=64)
@@ -119,7 +148,7 @@ def tile_routed_moe_kernel(tc, xT, w1, w2, gate, offs, out):
             nc.vector.tensor_copy(slot_scales[s][:], x_scales[:].indirect(offs_t[:, cols]))
 
         def layer1(e):
-            h_psum[e] = psum.tile([P, 4, C], F32, name="h_psum", tag="h_psum")
+            h_psum[e] = psum_h.tile([P, 4, C], F32, name="h_psum", tag="h_psum")
             cols = slice(C * (e % 4), C * (e % 4 + 1))
             for t in range(4):
                 for g in range(PASSES):
@@ -151,7 +180,7 @@ def tile_routed_moe_kernel(tc, xT, w1, w2, gate, offs, out):
             nc.vector.quantize_mx(out=hc[e][:].bitcast(FP8X4), scales=hs[e][:], in_=hb[e][:].rearrange("p n t -> p (n t)"))
 
         def layer2(e, n):
-            y_psum[e] = psum.tile([P, 2, C * n], F32, name="y_psum", tag="y_psum")
+            y_psum[e] = psum_y.tile([P, 2, C * n], F32, name="y_psum", tag="y_psum")
             for b in range(2):
                 for k in range(n):
                     codes, scales, at = w2_ops[e + k]
@@ -180,21 +209,32 @@ def tile_routed_moe_kernel(tc, xT, w1, w2, gate, offs, out):
                 MULT,
             )
 
-        xs = [[(("x", g, s), CFG["x"][2 * g + s])] for g in range(PASSES) for s in range(2)]
+        x_load = {}
+        xs = []
+        for a in range(PASSES):
+            pieces = CFG["x0"] if a == 0 else [CFG["xw"]] * (T // CFG["xw"])
+            x_load[a] = {sum(pieces[:k]): n for k, n in enumerate(pieces)}
+            c = 0
+            for n in pieces:
+                q = min(n, 512)
+                for k in range(n // q):
+                    xs.append([(("x", a, c, q), CFG["x"][2 * a + (1 if c >= 512 else 0)])])
+                    c += q
         weights = []
         for pair in range(E // 2):
             last = pair == E // 2 - 1
             share = CFG["w1_tail"] if last else CFG["w1"]
             tiles = [(("w1", 2 * pair + q // 3, q % 3), share[q]) for q in range(6)]
-            weights += [tiles[0:2], tiles[2:4]] + ([tiles[4:5], tiles[5:6]] if last else [tiles[4:6]])
+            if not last:
+                weights += [tiles[0:2], tiles[2:4], tiles[4:6]]
         for pair in reversed(range(E // 2 - 1)):
             weights.insert(min(3 * (pair + 1) + CFG["w2d"], len(weights)), [(("w2", 2 * pair, 2), CFG["w2"])])
-        n = len(weights)
-        if CFG["w2pos"][0] == CFG["w2pos"][1]:
-            weights.insert(n - CFG["w2pos"][0], [(("w2", E - 2, 2), CFG["w2_tail"][1])])
-        else:
-            weights.insert(n - CFG["w2pos"][0], [(("w2", E - 2, 1), CFG["w2_tail"][0])])
-            weights.insert(n + 1 - CFG["w2pos"][1], [(("w2", E - 1, 1), CFG["w2_tail"][1])])
+        w2a = [(("w2", E - 2, 1), CFG["w2_tail"][0])]
+        w2b = [(("w2", E - 1, 1), CFG["w2_tail"][1])]
+        tail = [tiles[0:2], tiles[2:4], tiles[4:5], tiles[5:6], w2a, w2b]
+        if CFG["split"]:
+            tail = [tiles[0:2], tiles[2:3], tiles[3:4], tiles[4:5], tiles[5:6], w2a, w2b]
+        weights += [tail[k] for k in CFG["order"] if k < len(tail)]
         first = CFG["first"]
         groups = weights[:first] + xs + weights[first:]
 
@@ -216,8 +256,8 @@ def tile_routed_moe_kernel(tc, xT, w1, w2, gate, offs, out):
                 d[2](*d[3])
 
         def follow(i, group):
-            kind, a, b = group[-1][0]
-            if kind == "x" and b == 1:
+            kind, a, b = group[-1][0][:3]
+            if kind == "x" and b + group[-1][0][3] == T:
                 gather_codes(a, 0)
                 if a == PASSES - 1:
                     gather_scales(0)
@@ -249,18 +289,24 @@ def tile_routed_moe_kernel(tc, xT, w1, w2, gate, offs, out):
         queue = []
         for group in groups:
             kind = group[0][0][0]
-            width = 512 if kind != "w2" else 256 * group[0][0][2]
+            width = {"x": group[0][0][-1], "w1": 512, "w2": 256 * group[0][0][2]}[kind]
             grouped = grp.tile([P, 4096], BF16, name="grouped", tag="grouped", align_bytes=64)
+            group_raw = load(group)
             for k, (job, share) in enumerate(group):
-                load_and_group(job, share, grouped, 2048 * k, width)
+                load_and_group(job, share, grouped, 2048 * k, width, group_raw)
+                if CFG["gpe"] and i == CFG["gpos"][0]:
+                    for k in range(2):
+                        spread = psum_y.tile([P, 512], F32, name="spread", tag="y_psum")
+                        nc.tensor.matmul(spread[:], pick[:], gate_row[:, 512 * k : 512 * (k + 1)], start=True, stop=True)
+                        nc.scalar.copy(gate_t[:, 512 * k : 512 * (k + 1)], spread[:])
                 for pair in range(E // 2):
-                    if i == CFG["gpos"][pair]:
+                    if i == CFG["gpos"][pair] and not CFG["gpe"]:
                         cols = slice(2 * C * pair, 2 * C * (pair + 1))
                         nc.sync.dma_start(gate_t[:, cols], gate[0:P, cols])
                 if len(queue) > CFG["qd"]:
                     g = queue.pop(0)
                     quantise(*g)
-                    if g[0][0][0] == ("x", PASSES - 1, 1):
+                    if g[0][0][0][0] == "x" and g[0][0][0][1] == PASSES - 1 and g[0][0][0][2] + g[0][0][0][3] == T:
                         x_ready[0] = 1
                     run_due(i)
                     follow(i, g[0])

@@ -15,7 +15,7 @@ FP8X4 = mybir.dt.float8_e4m3fn_x4
 MULT = mybir.AluOpType.mult
 RELU = mybir.ActivationFunctionType.Relu
 
-CFG = {"x": [0.5,0.375,0.625,0.375,0.125,0.375],"w1": [1,1,0.6875,1,0.3125,0],"w1_tail": [0.625,1,1,1,0.4375,1],"w2": 1,"w2_tail": [1,1],"relu": 0,"qh": 2,"l2": 4,"yc": 4,"sc": 8,"trelu": 1,"tqh": 1,"tl2": 2,"tyc": 3,"tsc": 5,"g1": [5,6,8,8],"first": 0,"qd": 0,"rawb": 10,"gpos": [15,24,28,21],"w2d": 0,"yV": 1,"tyV": 0,"rV": [0,1],"trV": [0,0],"hb": 4,"gpe": 1,"split": 0,"order": [0,1,4,2,3,5],"lw": 1,"x0": [256,256,512],"xw": 1024,"w2one": 1}
+CFG = {"x": [0.1875,0.5,1,0.0625,0.0625,0.375],"w1": [0.0625,1,0.5625,1,0.75,0],"w1_tail": [0.5625,1,1,0.3125,1,0.625],"w2": 0.5,"w2_tail": [0.625,0.625],"relu": 0,"qh": 3,"l2": 3,"yc": 3,"sc": 4,"trelu": 1,"tqh": 1,"tl2": 2,"tyc": 2,"tsc": 3,"g1": [5,10,0,6],"first": 0,"qd": 0,"rawb": 10,"gpos": [16,28,31,12],"w2d": 0,"yV": 1,"tyV": 0,"rV": [0,0],"trV": [1,1],"hb": 4,"gpe": 1,"split": 1,"order": [0,1,2,3,4,5,6],"lw": 1,"x0": [512,512],"xw": 512,"w2one": 1,"late2": 0}
 P = 128
 PASSES = K // 512
 HALF = 512
@@ -227,14 +227,16 @@ def tile_routed_moe_kernel(tc, xT, w1, w2, gate, offs, out):
             tiles = [(("w1", 2 * pair + q // 3, q % 3), share[q]) for q in range(6)]
             if not last:
                 weights += [tiles[0:2], tiles[2:4], tiles[4:6]]
-        for pair in reversed(range(E // 2 - 1)):
+        for pair in reversed(range(E // 2 - 1 - CFG["late2"])):
             weights.insert(min(3 * (pair + 1) + CFG["w2d"], len(weights)), [(("w2", 2 * pair, 2), CFG["w2"])])
         w2a = [(("w2", E - 2, 1), CFG["w2_tail"][0])]
         w2b = [(("w2", E - 1, 1), CFG["w2_tail"][1])]
         tail = [tiles[0:2], tiles[2:4], tiles[4:5], tiles[5:6], w2a, w2b]
         if CFG["split"]:
             tail = [tiles[0:2], tiles[2:3], tiles[3:4], tiles[4:5], tiles[5:6], w2a, w2b]
-        weights += [tail[k] for k in CFG["order"] if k < len(tail)]
+        if CFG["late2"]:
+            tail.append([(("w2", E - 4, 2), CFG["w2"])])
+        weights += [tail[k] for k in CFG["order"]]
         first = CFG["first"]
         groups = weights[:first] + xs + weights[first:]
 

@@ -15,7 +15,7 @@ FP8X4 = mybir.dt.float8_e4m3fn_x4
 MULT = mybir.AluOpType.mult
 RELU = mybir.ActivationFunctionType.Relu
 
-CFG = {"x": [0.1875,0.5,1,0.0625,0.0625,0.375],"w1": [0.0625,1,0.5625,1,0.75,0],"w1_tail": [0.5625,1,1,0.3125,1,0.625],"w2": 0.5,"w2_tail": [0.625,0.625],"relu": 0,"qh": 3,"l2": 3,"yc": 3,"sc": 4,"trelu": 1,"tqh": 1,"tl2": 2,"tyc": 2,"tsc": 3,"g1": [5,10,0,6],"first": 0,"qd": 0,"rawb": 10,"gpos": [16,28,31,12],"w2d": 0,"yV": 1,"tyV": 0,"rV": [0,0],"trV": [1,1],"hb": 4,"gpe": 1,"split": 1,"order": [0,1,2,3,4,5,6],"lw": 1,"x0": [512,512],"xw": 512,"w2one": 1,"late2": 0}
+CFG = {"x": [0.25,0.5,1,0,0,0.5],"w1": [0,1,0.5,1,0.75,0],"w1_tail": [0.5,1,1,0.25,1,0.625],"w2": 0.5,"w2_tail": [0.625,0.625],"relu": 0,"qh": 3,"l2": 3,"yc": 3,"sc": 4,"trelu": 1,"tqh": 1,"tl2": 2,"tyc": 2,"tsc": 3,"g1": [5,10,0,6],"first": 0,"qd": 0,"rawb": 10,"gpos": [16,0,0,0],"w2d": 0,"yV": 1,"tyV": 0,"rV": [0,0],"trV": [1,1],"hb": 4,"gpe": 1,"split": 1,"order": [0,1,2,3,4,5,6],"lw": 1,"x0": [512,512],"xw": 512,"w2one": 1,"late2": 0}
 P = 128
 PASSES = K // 512
 HALF = 512
@@ -35,11 +35,9 @@ def tile_routed_moe_kernel(tc, xT, w1, w2, gate, offs, out):
         psum_y = ctx.enter_context(tc.psum_pool(name="psum_y", bufs=3))
 
         offs_t = keep.tile([P, E * C // 16], U16, name="offs_t")
-        nc.sync.dma_start(offs_t[:], offs)
         if CFG["gpe"]:
             gate_row = keep.tile([P, E * C], F32, name="gate_row")
             nc.gpsimd.memset(gate_row[:], 0.0)
-            nc.sync.dma_start(gate_row[0:1, :], gate[0:1, :])
             pick = keep.tile([P, P], F32, name="pick")
             nc.gpsimd.memset(pick[:], 0.0)
             nc.gpsimd.memset(pick[0:1, :], 1.0)
@@ -296,6 +294,9 @@ def tile_routed_moe_kernel(tc, xT, w1, w2, gate, offs, out):
             group_raw = load(group)
             for k, (job, share) in enumerate(group):
                 load_and_group(job, share, grouped, 2048 * k, width, group_raw)
+                if i == 0:
+                    nc.sync.dma_start(offs_t[:], offs)
+                    nc.sync.dma_start(gate_row[0:1, :], gate[0:1, :])
                 if CFG["gpe"] and i == CFG["gpos"][0]:
                     for k in range(2):
                         spread = psum_y.tile([P, 512], F32, name="spread", tag="y_psum")

from contextlib import ExitStack

import concourse.mybir as mybir

K, T, E, C, H, N = 1536, 1024, 8, 128, 512, 256
FLOPS = 2 * E * C * (K * H + H * N)
BYTES = 4 * (K * T + E * K * H + E * H * N + E * C + N * T) + 2 * E * C

F32 = mybir.dt.float32
BF16 = mybir.dt.bfloat16
U32 = mybir.dt.uint32
U16 = mybir.dt.uint16
U8 = mybir.dt.uint8
FP8X4 = mybir.dt.float8_e4m3fn_x4
MULT = mybir.AluOpType.mult
RELU = mybir.ActivationFunctionType.Relu

CFG = {"x": [0.25,0.5,1,0,0,0.5],"w1": [0,1,0.5,1,0.75,0],"w1_tail": [0.5,1,1,0.25,1,0.625],"w2": 0.5,"w2_tail": [0.625,0.625],"relu": 0,"qh": 3,"l2": 3,"yc": 3,"sc": 4,"trelu": 1,"tqh": 1,"tl2": 2,"tyc": 2,"tsc": 3,"g1": [5,10,0,6],"first": 0,"qd": 0,"rawb": 10,"gpos": [16,0,0,0],"w2d": 0,"yV": 1,"tyV": 0,"rV": [0,0],"trV": [1,1],"hb": 4,"gpe": 1,"split": 1,"order": [0,1,2,3,4,5,6],"lw": 1,"x0": [512,512],"xw": 512,"w2one": 1,"late2": 0}
P = 128
PASSES = K // 512
HALF = 512


def tile_routed_moe_kernel(tc, xT, w1, w2, gate, offs, out):
    nc = tc.nc
    with ExitStack() as ctx:
        keep = ctx.enter_context(tc.tile_pool(name="keep", bufs=1))
        rawp = ctx.enter_context(tc.tile_pool(name="rawp", bufs=CFG["rawb"]))
        rawxp = ctx.enter_context(tc.tile_pool(name="rawxp", bufs=2))
        grp = ctx.enter_context(tc.tile_pool(name="grp", bufs=4))
        w1p = ctx.enter_context(tc.tile_pool(name="w1p", bufs=5))
        w2p = ctx.enter_context(tc.tile_pool(name="w2p", bufs=2))
        hp = ctx.enter_context(tc.tile_pool(name="hp", bufs=2))
        psum_h = ctx.enter_context(tc.psum_pool(name="psum_h", bufs=CFG["hb"]))
        psum_y = ctx.enter_context(tc.psum_pool(name="psum_y", bufs=3))

        offs_t = keep.tile([P, E * C // 16], U16, name="offs_t")
        if CFG["gpe"]:
            gate_row = keep.tile([P, E * C], F32, name="gate_row")
            nc.gpsimd.memset(gate_row[:], 0.0)
            pick = keep.tile([P, P], F32, name="pick")
            nc.gpsimd.memset(pick[:], 0.0)
            nc.gpsimd.memset(pick[0:1, :], 1.0)
        gate_t = keep.tile([P, E * C], F32, name="gate_t")
        window = [keep.tile([P, T], F32, name=f"window{b}") for b in range(2)]
        x_codes = [keep.tile([P, T], U32, name=f"x_codes{g}", align_bytes=64) for g in range(PASSES)]
        x_scales = keep.tile([P, T], U8, name="x_scales", align_bytes=64)
        nc.gpsimd.memset(x_scales[:], 0)
        slot_codes = [[keep.tile([P, HALF], U32, name=f"slot_codes{g}_{s}", align_bytes=64) for s in range(2)] for g in range(PASSES)]
        slot_scales = [keep.tile([P, HALF], U8, name=f"slot_scales{s}", align_bytes=64) for s in range(2)]

        x_raw, w1_ops, w2_ops = {}, {}, {}
        h_psum, y_psum, y_sb, hb, hc, hs = {}, {}, {}, {}, {}, {}

        def load(group):
            kind, a, b = group[0][0][:3]
            if kind == "x":
                if b not in x_load[a]:
                    return x_raw[a, b][0][:, :, x_raw[a, b][1] : x_raw[a, b][1] + group[0][0][3]]
                n = x_load[a][b]
                pool = rawp if n <= 512 or CFG["lw"] == 2 else rawxp
                raw = pool.tile([P, 4, n], F32, name="raw", tag="raw")
                nc.sync.dma_start(raw[:], xT[512 * a : 512 * (a + 1), b : b + n].rearrange("(p j) n -> p j n", j=4))
                for c in range(b, b + n, 256):
                    x_raw[a, c] = (raw, c - b)
                return raw[:, :, 0 : group[0][0][3]]
            if kind == "w1":
                raws = []
                step = CFG["lw"] if len(group) == 2 else 1
                for k in range(0, len(group), step):
                    raw = rawp.tile([P, step, 4, 512], F32, name="raw", tag="raw")
                    row = 512 * (PASSES * a + b + k)
                    nc.sync.dma_start(raw[:], w1.rearrange("e k n -> (e k) n")[row : row + 512 * step, :].rearrange("(u p j) n -> p u j n", u=step, j=4))
                    raws += [raw[:, u] for u in range(step)]
                return raws
            if kind == "w2":
                raw = rawp.tile([P, b * 1024], F32, name="raw", tag="raw")
                nc.sync.dma_start(raw[:].rearrange("p (e m) -> p e m", e=b), w2[a : a + b].rearrange("e (p j) n -> p e (j n)", j=4))
                return raw
            return None

        def load_and_group(job, share, grouped, at, width, group_raw):
            kind, a, b = job[:3]
            if kind == "x":
                raw = group_raw
            elif kind == "w1":
                raw = group_raw[at // 2048]
            else:
                raw = group_raw[:, :]
            whole = grouped[:, at : at + 4 * width]
            if kind == "w1":
                dst = whole.rearrange("p (t m j) -> p m j t", t=4, j=4)
                src = raw[:, :, :].rearrange("p j (m t) -> p m j t", t=4)
            elif kind == "x":
                dst = whole.rearrange("p (c i j) -> p c j i", i=4, j=4)
                src = raw[:, :, :].rearrange("p j (c i) -> p c j i", i=4)
            else:
                dst = whole.rearrange("p (e c i j) -> p e c j i", e=b, i=4, j=4)
                src = raw[:].rearrange("p (e j c i) -> p e c j i", e=b, i=4, j=4)
                if share == 0.5 and b == 2:
                    nc.scalar.copy(dst[:, 0], src[:, 0])
                    nc.vector.tensor_copy(dst[:, 1], src[:, 1])
                    return
                if share in (0.0, 1.0) and CFG["w2one"]:
                    copy = nc.scalar.copy if share else nc.vector.tensor_copy
                    copy(dst, src)
                    return
                for k in range(b):
                    cut = int(64 * share) // 4 * 4
                    if cut > 0:
                        nc.scalar.copy(dst[:, k, :cut], src[:, k, :cut])
                    if cut < 64:
                        nc.vector.tensor_copy(dst[:, k, cut:], src[:, k, cut:])
                return
            cut = int(width // 4 * share) // 4 * 4
            if cut > 0:
                nc.scalar.copy(dst[:, :cut], src[:, :cut])
            if cut < width // 4:
                nc.vector.tensor_copy(dst[:, cut:], src[:, cut:])

        def quantise(group, grouped, width):
            kind, a, b = group[0][0][:3]
            if kind == "x":
                cols = slice(b, b + width)
                codes, scales = x_codes[a][:, cols], x_scales[4 * a : P, cols]
            elif kind == "w1":
                codes = w1p.tile([P, width], U32, name="w1_codes", tag="w1_codes", align_bytes=64)
                scales = w1p.tile([P, width], U8, name="w1_scales", tag="w1_scales", align_bytes=64)
                for k, (job, share) in enumerate(group):
                    w1_ops[job[1], job[2]] = (codes, scales, 512 * k)
                codes, scales = codes[:], scales[:]
            else:
                codes = w2p.tile([P, width], U32, name="w2_codes", tag="w2_codes", align_bytes=64)
                scales = w2p.tile([P, width], U8, name="w2_scales", tag="w2_scales", align_bytes=64)
                for k in range(b):
                    w2_ops[a + k] = (codes, scales, 256 * k)
                codes, scales = codes[:], scales[:]
            nc.vector.quantize_mx(out=codes.bitcast(FP8X4), scales=scales, in_=grouped[:, : 4 * width])

        def gather_codes(g, s):
            cols = slice(HALF // 16 * s, HALF // 16 * (s + 1))
            nc.vector.tensor_copy(slot_codes[g][s][:], x_codes[g][:].indirect(offs_t[:, cols]))

        def gather_scales(s):
            cols = slice(HALF // 16 * s, HALF // 16 * (s + 1))
            nc.vector.tensor_copy(slot_scales[s][:], x_scales[:].indirect(offs_t[:, cols]))

        def layer1(e):
            h_psum[e] = psum_h.tile([P, 4, C], F32, name="h_psum", tag="h_psum")
            cols = slice(C * (e % 4), C * (e % 4 + 1))
            for t in range(4):
                for g in range(PASSES):
                    codes, scales, at = w1_ops[e, g]
                    nc.tensor.matmul_mx(
                        out=h_psum[e][:, t, :],
                        lhsT=codes[:, at + 128 * t : at + 128 * (t + 1)].bitcast(FP8X4),
                        lhsT_scale=scales[:, at + 128 * t : at + 128 * (t + 1)],
                        rhs=slot_codes[g][e // 4][:, cols].bitcast(FP8X4),
                        rhs_scale=slot_scales[e // 4][4 * g : P, cols],
                        start=(g == 0),
                        stop=(g == PASSES - 1),
                    )

        def hidden(e, n):
            if e % n == 0:
                hb[e] = hp.tile([P, C * n, 4], BF16, name="hb", tag="hb", align_bytes=64)
            k = e % n
            dst = hb[e - k][:, C * k : C * (k + 1), :]
            src = h_psum[e][:].rearrange("p t n -> p n t")
            if CFG["trV" if e >= E - 2 else "rV"][e % 2]:
                nc.vector.tensor_scalar_max(dst, src, 0.0)
            else:
                nc.scalar.activation(dst, src, RELU)

        def quantise_hidden(e, n):
            hc[e] = hp.tile([P, C * n], U32, name="hc", tag="hc", align_bytes=64)
            hs[e] = hp.tile([P, C * n], U8, name="hs", tag="hs", align_bytes=64)
            nc.vector.quantize_mx(out=hc[e][:].bitcast(FP8X4), scales=hs[e][:], in_=hb[e][:].rearrange("p n t -> p (n t)"))

        def layer2(e, n):
            y_psum[e] = psum_y.tile([P, 2, C * n], F32, name="y_psum", tag="y_psum")
            for b in range(2):
                for k in range(n):
                    codes, scales, at = w2_ops[e + k]
                    nc.tensor.matmul_mx(
                        out=y_psum[e][:, b, C * k : C * (k + 1)],
                        lhsT=codes[:, at + 128 * b : at + 128 * (b + 1)].bitcast(FP8X4),
                        lhsT_scale=scales[:, at + 128 * b : at + 128 * (b + 1)],
                        rhs=hc[e][:, C * k : C * (k + 1)].bitcast(FP8X4),
                        rhs_scale=hs[e][:, C * k : C * (k + 1)],
                        start=True,
                        stop=True,
                    )

        def y_out(e, n):
            y_sb[e] = hp.tile([P, 2, C * n], F32, name="y_sb", tag="y_sb")
            if CFG["tyV" if e >= E - 2 else "yV"]:
                nc.vector.tensor_copy(y_sb[e][:], y_psum[e][:])
            else:
                nc.scalar.copy(y_sb[e][:], y_psum[e][:])

        def scatter(e, n, b):
            nc.vector.tensor_tensor(
                window[b][:].indirect(offs_t[:, C // 16 * e : C // 16 * (e + n)]),
                y_sb[e][:, b, :],
                gate_t[:, C * e : C * (e + n)],
                MULT,
            )

        x_load = {}
        xs = []
        for a in range(PASSES):
            pieces = CFG["x0"] if a == 0 else [CFG["xw"]] * (T // CFG["xw"])
            x_load[a] = {sum(pieces[:k]): n for k, n in enumerate(pieces)}
            c = 0
            for n in pieces:
                q = min(n, 512)
                for k in range(n // q):
                    xs.append([(("x", a, c, q), CFG["x"][2 * a + (1 if c >= 512 else 0)])])
                    c += q
        weights = []
        for pair in range(E // 2):
            last = pair == E // 2 - 1
            share = CFG["w1_tail"] if last else CFG["w1"]
            tiles = [(("w1", 2 * pair + q // 3, q % 3), share[q]) for q in range(6)]
            if not last:
                weights += [tiles[0:2], tiles[2:4], tiles[4:6]]
        for pair in reversed(range(E // 2 - 1 - CFG["late2"])):
            weights.insert(min(3 * (pair + 1) + CFG["w2d"], len(weights)), [(("w2", 2 * pair, 2), CFG["w2"])])
        w2a = [(("w2", E - 2, 1), CFG["w2_tail"][0])]
        w2b = [(("w2", E - 1, 1), CFG["w2_tail"][1])]
        tail = [tiles[0:2], tiles[2:4], tiles[4:5], tiles[5:6], w2a, w2b]
        if CFG["split"]:
            tail = [tiles[0:2], tiles[2:3], tiles[3:4], tiles[4:5], tiles[5:6], w2a, w2b]
        if CFG["late2"]:
            tail.append([(("w2", E - 4, 2), CFG["w2"])])
        weights += [tail[k] for k in CFG["order"]]
        first = CFG["first"]
        groups = weights[:first] + xs + weights[first:]

        due = []
        count = [0]
        done = {}

        def at(i, f, *args):
            count[0] += 1
            due.append((i, count[0], f, args))

        def run_due(i):
            while True:
                ready = sorted(d for d in due if d[0] <= i)
                if not ready:
                    return
                d = ready[0]
                due.remove(d)
                d[2](*d[3])

        def follow(i, group):
            kind, a, b = group[-1][0][:3]
            if kind == "x" and b + group[-1][0][3] == T:
                gather_codes(a, 0)
                if a == PASSES - 1:
                    gather_scales(0)
                    for k in range(3):
                        at(i + CFG["g1"][k], gather_codes, k, 1)
                    at(i + CFG["g1"][3], gather_scales, 1)
            for e in range(E):
                tail = e >= E - 2
                t = "t" if tail else ""
                width = 1 if tail else 2
                lead = e if tail else e // 2 * 2
                if all((e, g) in w1_ops for g in range(PASSES)) and ("l1", e) not in done and x_ready[0]:
                    done["l1", e] = i + CFG[t + "relu"]
                    layer1(e)
                    at(done["l1", e], hidden, e, width)
                    if e == lead + width - 1:
                        done["q", lead] = i + CFG[t + "qh"]
                        at(i + CFG[t + "qh"], quantise_hidden, lead, width)
                if ("q", lead) in done and all(lead + k in w2_ops for k in range(width)) and ("l2", lead) not in done:
                    base = max(i, done["q", lead])
                    done["l2", lead] = base
                    at(base + CFG[t + "l2"] - CFG[t + "qh"], layer2, lead, width)
                    at(base + CFG[t + "yc"] - CFG[t + "qh"], y_out, lead, width)
                    at(base + CFG[t + "sc"] - CFG[t + "qh"], scatter, lead, width, 0)
                    at(base + CFG[t + "sc"] - CFG[t + "qh"], scatter, lead, width, 1)

        x_ready = [0]
        i = 0
        queue = []
        for group in groups:
            kind = group[0][0][0]
            width = {"x": group[0][0][-1], "w1": 512, "w2": 256 * group[0][0][2]}[kind]
            grouped = grp.tile([P, 4096], BF16, name="grouped", tag="grouped", align_bytes=64)
            group_raw = load(group)
            for k, (job, share) in enumerate(group):
                load_and_group(job, share, grouped, 2048 * k, width, group_raw)
                if i == 0:
                    nc.sync.dma_start(offs_t[:], offs)
                    nc.sync.dma_start(gate_row[0:1, :], gate[0:1, :])
                if CFG["gpe"] and i == CFG["gpos"][0]:
                    for k in range(2):
                        spread = psum_y.tile([P, 512], F32, name="spread", tag="y_psum")
                        nc.tensor.matmul(spread[:], pick[:], gate_row[:, 512 * k : 512 * (k + 1)], start=True, stop=True)
                        nc.scalar.copy(gate_t[:, 512 * k : 512 * (k + 1)], spread[:])
                for pair in range(E // 2):
                    if i == CFG["gpos"][pair] and not CFG["gpe"]:
                        cols = slice(2 * C * pair, 2 * C * (pair + 1))
                        nc.sync.dma_start(gate_t[:, cols], gate[0:P, cols])
                if len(queue) > CFG["qd"]:
                    g = queue.pop(0)
                    quantise(*g)
                    if g[0][0][0][0] == "x" and g[0][0][0][1] == PASSES - 1 and g[0][0][0][2] + g[0][0][0][3] == T:
                        x_ready[0] = 1
                    run_due(i)
                    follow(i, g[0])
                else:
                    run_due(i)
                i += 1
            queue.append((group, grouped, width * len(group)))
        for g in queue:
            quantise(*g)
            run_due(i)
            follow(i, g[0])
            i += 1
        run_due(1000)
        for b in range(2):
            nc.sync.dma_start(out[P * b : P * (b + 1), :], window[b][:])
